import numpy as np
import ml_dtypes


def mxq(x, axis, fmt="e4m3"):
    dtype, down = {"e4m3": (ml_dtypes.float8_e4m3fn, 7), "e5m2": (ml_dtypes.float8_e5m2, 14)}[fmt]
    v = np.moveaxis(np.asarray(x, np.float32).astype(ml_dtypes.bfloat16).astype(np.float64), axis, -1)
    blocks = v.reshape(v.shape[:-1] + (-1, 32))
    amax = np.abs(blocks).max(-1, keepdims=True)
    byte = np.maximum(np.where(amax > 0, np.frexp(amax)[1] - 1 + 127, 0) - down, 1)
    scale = np.exp2(byte - 127.0)
    codes = (blocks / scale).astype(np.float32).astype(dtype).astype(np.float64)
    return np.moveaxis((codes * scale).reshape(v.shape), -1, axis)


WIDE = False


def mx_kscale(k):
    if not WIDE:
        return np.ones(k)
    levels = np.array([10, -10, 5, -5, 0])
    if k % 512:
        return np.exp2(np.random.permutation(np.resize(levels, k // 32))).repeat(32)
    a = np.empty((k // 512, 16))
    for p in range(k // 512):
        a[p, :8] = np.random.permutation(np.resize(levels, 8))
        for g in range(8):
            far = levels[np.abs(levels - a[p, g]) >= 10]
            a[p, g + 8] = far[np.random.randint(len(far))]
    return np.exp2(a.ravel()).repeat(32)


def f64(x):
    return np.asarray(x).astype(np.float64)


def striped(idx):
    return np.tile(idx.reshape(-1, 16).T, (8, 1)).astype(np.uint16)


def unstriped(offs):
    return offs[:16].T.reshape(-1).astype(np.int64)


E2M1 = np.array([0.0, 0.5, 1.0, 1.5, 2.0, 3.0, 4.0, 6.0, -0.0, -0.5, -1.0, -1.5, -2.0, -3.0, -4.0, -6.0])


def pack_weight(w, fmt):
    k, n = w.shape
    w = f64(np.asarray(w, np.float32).astype(ml_dtypes.bfloat16)).reshape(k // 32, 32, n)
    amax = np.abs(w).max(1)
    if fmt == "e4m3":
        byte = np.frexp(amax)[1] - 1 + 127 - 7
    else:
        mant, ex = np.frexp(amax / 6.0)
        byte = np.where(mant > 0.5, ex, ex - 1) + 127
    byte = np.clip(np.where(amax > 0, byte, 1), 1, 254)
    scaled = (w * np.exp2(127.0 - byte)[:, None, :]).reshape(k, n).astype(np.float32)
    by_word = np.ascontiguousarray(scaled.reshape(k // 512, 128, 4, n).transpose(0, 1, 3, 2))
    if fmt == "e4m3":
        words = by_word.astype(ml_dtypes.float8_e4m3fn).view(np.uint8)
    else:
        c = by_word.astype(ml_dtypes.float4_e2m1fn).view(np.uint8) & 0xF
        words = (c[..., 0::2] | (c[..., 1::2] << 4)).reshape(k // 512, 128, 2 * n)
    return np.ascontiguousarray(words), np.ascontiguousarray(byte.astype(np.uint8).reshape(k // 512, 16, n))


def unpack_weight(words, scales, fmt):
    g, _, n = scales.shape
    words = np.ascontiguousarray(words).reshape(g, 128, n, -1)
    if fmt == "e4m3":
        vals = words.view(ml_dtypes.float8_e4m3fn).astype(np.float64)
    else:
        nib = np.empty((g, 128, n, 4), np.uint8)
        nib[..., 0::2] = words & 0xF
        nib[..., 1::2] = words >> 4
        vals = E2M1[nib]
    vals = vals * np.repeat(np.exp2(scales.astype(np.float64) - 127.0), 8, axis=1)[..., None]
    return vals.transpose(0, 1, 3, 2).reshape(g * 512, n)


def pack_table4(v):
    words, scales = pack_weight(v, "e2m1")
    g, t = words.shape[0] // 2, v.shape[1]
    words = words.reshape(g, 2, 128, t, 2).transpose(0, 2, 3, 1, 4)
    return np.concatenate([words.reshape(g, -1), scales.reshape(g, -1)], axis=1)


def unpack_table4(tab):
    g, t = tab.shape[0], tab.shape[1] // 544
    words = tab[:, :512 * t].reshape(g, 128, t, 2, 2).transpose(0, 3, 1, 2, 4).reshape(2 * g, 128, 2 * t)
    return unpack_weight(words, tab[:, 512 * t:].reshape(2 * g, 16, t), "e2m1")


def pack_table(v):
    words, scales = pack_weight(v, "e4m3")
    return np.concatenate([words.reshape(words.shape[0], -1), scales.reshape(scales.shape[0], -1)], axis=1)


def unpack_table(tab):
    g, t = tab.shape[0], tab.shape[1] // 528
    return unpack_weight(tab[:, :512 * t].reshape(g, 128, t, 4), tab[:, 512 * t:].reshape(g, 16, t), "e4m3")


def gelu(v):
    return 0.5 * v * (1.0 + np.tanh(np.sqrt(2.0 / np.pi) * (v + 0.044715 * v**3)))


K, L, M, T, S = 1024, 1024, 128, 2048, 1024


def setup_inputs():
    n = np.random.standard_normal
    s1 = mx_kscale(K)[:, None]
    s2 = mx_kscale(L)[:, None]
    p_w4 = pack_weight(n((K, M)) / np.sqrt(K) / s1, "e2m1")
    return {
        "tab": pack_table(n((K, T)) * s1),
        "w4_words": p_w4[0],
        "w4_scales": p_w4[1],
        "tab2": pack_table4(n((L, T)) * s2),
        "u": (n((L, M)) / np.sqrt(L) / s2).astype(np.float32),
        "b": (0.3 * n(128)).astype(np.float32),
        "offs": striped(np.random.permutation(T)[:S]),
        "offs2": striped(np.random.permutation(T)[:S]),
    }


def reference(tab, w4_words, w4_scales, tab2, u, b, offs, offs2):
    tab_ = unpack_table(tab)[:, unstriped(offs)]
    w4_ = unpack_weight(w4_words, w4_scales, "e2m1")
    tab2_ = unpack_table4(tab2)[:, unstriped(offs2)]
    u_ = mxq(f64(u), 0, "e4m3")
    y = w4_.T @ tab_ + u_.T @ tab2_
    return gelu(y + f64(b)[:, None])

@@ -1,0 +1,142 @@
+from contextlib import ExitStack
+
+import concourse.mybir as mybir
+
+K, L, M, T, S = 1024, 1024, 128, 2048, 1024
+FLOPS = 2 * M * S * (K + L)
+
+F32 = mybir.dt.float32
+BF16 = mybir.dt.bfloat16
+I32 = mybir.dt.int32
+U32 = mybir.dt.uint32
+U16 = mybir.dt.uint16
+U8 = mybir.dt.uint8
+FP8X4 = mybir.dt.float8_e4m3fn_x4
+FP4X4 = mybir.dt.float4_e2m1fn_x4
+GELU = mybir.ActivationFunctionType.Gelu_apprx_tanh
+
+P = 128
+WORD_BYTES = 512 * T
+
+
+def tile_list_tab48_gelu_kernel(tc, tab, w4_words, w4_scales, tab2, u, b, offs, offs2, out):
+    nc = tc.nc
+    with ExitStack() as ctx:
+        keep = ctx.enter_context(tc.tile_pool(name="keep", bufs=1))
+        psum = ctx.enter_context(tc.psum_pool(name="psum", bufs=1))
+
+        lst = keep.tile([P, S // 16], U16, name="lst")
+        lst2 = keep.tile([P, S // 16], U16, name="lst2")
+        sc = [keep.tile([P, T // 4], I32, name=f"sc{a}", align_bytes=64) for a in range(2)]
+        words = [keep.tile([P, T], I32, name=f"words{a}", align_bytes=64) for a in range(2)]
+        sc2 = keep.tile([P, T // 4], I32, name="sc2", align_bytes=64)
+        words2 = keep.tile([P, T], I32, name="words2", align_bytes=64)
+        u_raw = keep.tile([P, 2, 4, M], F32, name="u_raw", align_bytes=64)
+        u_bf = keep.tile([P, 2, M, 4], BF16, name="u_bf", align_bytes=64)
+        u_codes = keep.tile([P, 2 * M], U32, name="u_codes", align_bytes=64)
+        u_scales = keep.tile([P, 2 * M], U8, name="u_scales", align_bytes=64)
+        w4 = keep.tile([P, 2, M // 2], I32, name="w4", align_bytes=64)
+        w4_sc = keep.tile([P, 2, M // 4], I32, name="w4_sc", align_bytes=64)
+        bias = keep.tile([P, 1], F32, name="bias")
+        warm = keep.tile([P, 1], F32, name="warm")
+
+        g_words = [keep.tile([P, S], U32, name=f"g_words{a}", align_bytes=64) for a in range(2)]
+        g_sc = [keep.tile([P, S], U8, name=f"g_sc{a}", align_bytes=64) for a in range(2)]
+        g_words2 = keep.tile([P, S], U32, name="g_words2", align_bytes=64)
+        g_parted = keep.tile([P, 2 * 2 * S], U8, name="g_parted", align_bytes=64)
+        g_sc2 = [keep.tile([P, S // 4], I32, name=f"g_sc2_{h}", align_bytes=64) for h in range(2)]
+
+        nc.vector.memset(sc[0][:], 0)
+        nc.vector.memset(sc[1][:], 0)
+        nc.gpsimd.memset(warm[:], 0.0)
+        nc.gpsimd.memset(sc2[:], 0)
+        nc.gpsimd.memset(g_sc2[1][:], 0)
+        nc.gpsimd.memset(w4_sc[:], 0)
+        nc.scalar.activation(out=warm[:], in_=warm[:], func=GELU)
+
+        def load_words(dst, row, eng):
+            eng.dma_start(out=dst[:], in_=row.rearrange("(p b) -> p b", b=4 * T).bitcast(I32))
+
+        def load_scales(dst, row, q, k0, row0, eng):
+            lo = WORD_BYTES + T * (row0 + 4 * q)
+            eng.dma_start(out=dst[32 * q + k0 : 32 * q + k0 + 4, :], in_=row[lo : lo + 4 * T].rearrange("(r b) -> r b", b=T).bitcast(I32))
+
+        nc.sync.dma_start(lst[:], offs)
+        for q in range(4):
+            load_scales(sc[0], tab[0], q, 0, 0, nc.sync)
+        nc.sync.dma_start(out=u_raw[:], in_=u.rearrange("(a p j) n -> p a j n", a=2, j=4))
+        load_words(words[0], tab[0, 0:WORD_BYTES], nc.sync)
+        for q in range(4):
+            load_scales(sc[1], tab[1], q, 0, 0, nc.sync)
+        nc.sync.dma_start(lst2[:], offs2)
+        load_words(words2, tab2[0, 0:WORD_BYTES], nc.sync)
+        for h in range(2):
+            for q in range(4):
+                load_scales(sc2, tab2[0], q, 4 * h, 16 * h, nc.sync)
+        load_words(words[1], tab[1, 0:WORD_BYTES], nc.sync)
+        nc.scalar.dma_start(out=w4[:], in_=w4_words.rearrange("a p c -> p a c").bitcast(I32))
+        for q in range(4):
+            nc.scalar.dma_start(out=w4_sc[32 * q : 32 * q + 4, :, :], in_=w4_scales[:, 4 * q : 4 * q + 4, :].rearrange("a r n -> r a n").bitcast(I32))
+        nc.scalar.dma_start(out=bias[:], in_=b.rearrange("(p o) -> p o", o=1))
+
+        for a in range(2):
+            nc.scalar.copy(out=u_bf[:, a, :, :], in_=u_raw[:, a, :, :].rearrange("p j n -> p n j"))
+
+        def gather(dst, window, offsets):
+            nc.vector.tensor_copy(dst, window.indirect(offsets))
+
+        gather(g_sc[0][:], sc[0][:].bitcast(U8), lst[:])
+        gather(g_words[0][:], words[0][:].bitcast(U32), lst[:])
+        nc.vector.quantize_mx(out=u_codes[:].bitcast(FP8X4), scales=u_scales[:], in_=u_bf[:].rearrange("p a n j -> p (a n j)"))
+        gather(g_words2[:], words2[:].bitcast(U32), lst2[:])
+        gather(g_sc2[0][:].bitcast(U8), sc2[:].bitcast(U8), lst2[:])
+        for q in range(4):
+            nc.sync.dma_start(out=g_sc2[1][32 * q : 32 * q + 4, :], in_=g_sc2[0][32 * q + 4 : 32 * q + 8, :])
+        nc.vector.tensor_copy(
+            out=g_parted[:].bitcast(U16).rearrange("p (h n) -> p h n", h=2),
+            in_=g_words2[:].bitcast(U16).rearrange("p (n h) -> p h n", h=2),
+        )
+        gather(g_sc[1][:], sc[1][:].bitcast(U8), lst[:])
+        pieces = ((0, 512), (512, 768), (768, 1024))
+        for lo, hi in pieces:
+            gather(g_words[1][:, lo:hi], words[1][:].bitcast(U32), lst[:, lo // 16 : hi // 16])
+
+        groups = [(0, 512)] + [(lo, lo + 128) for lo in range(512, 1024, 128)]
+        w4_u8 = w4[:].rearrange("p a c -> p (a c)").bitcast(U8)
+        w4_sc_u8 = w4_sc[:].rearrange("p a c -> p (a c)").bitcast(U8)
+        acc = [psum.tile([M, hi - lo], F32, name=f"acc{lo}") for lo, hi in groups]
+
+        def mm_w4(i, a, start, stop):
+            lo, hi = groups[i]
+            nc.tensor.matmul_mx(
+                out=acc[i][:],
+                lhsT=w4_u8[:, 256 * a : 256 * a + 256].bitcast(FP4X4),
+                lhsT_scale=w4_sc_u8[:, M * a : M * a + M],
+                rhs=g_words[a][:, lo:hi].bitcast(FP8X4),
+                rhs_scale=g_sc[a][:, lo:hi],
+                start=start, stop=stop,
+            )
+
+        def mm_u(i, h):
+            lo, hi = groups[i]
+            nc.tensor.matmul_mx(
+                out=acc[i][:],
+                lhsT=u_codes[:, M * h : M * h + M].bitcast(FP8X4),
+                lhsT_scale=u_scales[:, M * h : M * h + M],
+                rhs=g_parted[:, 2 * S * h + 2 * lo : 2 * S * h + 2 * hi].bitcast(FP4X4),
+                rhs_scale=g_sc2[h][:].bitcast(U8)[:, lo:hi],
+                start=False, stop=False,
+            )
+
+        for i in range(len(groups)):
+            mm_w4(i, 0, True, False)
+        for h in range(2):
+            for i in range(len(groups)):
+                mm_u(i, h)
+        result = [keep.tile([M, hi - lo], F32, name=f"result{lo}") for lo, hi in pieces]
+        for t, (p_lo, p_hi) in enumerate(pieces):
+            for i, (lo, hi) in enumerate(groups):
+                if p_lo <= lo and hi <= p_hi:
+                    mm_w4(i, 1, False, True)
+                    nc.scalar.activation(out=result[t][:, lo - p_lo : hi - p_lo], in_=acc[i][:], func=GELU, bias=bias[:])
+            nc.sync.dma_start(out=out[:, p_lo:p_hi], in_=result[t][:])

@@ -27,7 +27,7 @@ def tile_list_tab48_gelu_kernel(tc, tab, w4_words, w4_scales, tab2, u, b, offs, 
 
         lst = keep.tile([P, S // 16], U16, name="lst")
         lst2 = keep.tile([P, S // 16], U16, name="lst2")
-        sc = [keep.tile([P, T // 4], I32, name=f"sc{a}", align_bytes=64) for a in range(2)]
+        sc = keep.tile([P, 2, T // 4], I32, name="sc", align_bytes=64)
         words = [keep.tile([P, T], I32, name=f"words{a}", align_bytes=64) for a in range(2)]
         sc2 = keep.tile([P, T // 4], I32, name="sc2", align_bytes=64)
         words2 = keep.tile([P, T], I32, name="words2", align_bytes=64)
@@ -44,40 +44,34 @@ def tile_list_tab48_gelu_kernel(tc, tab, w4_words, w4_scales, tab2, u, b, offs, 
         g_sc = [keep.tile([P, S], U8, name=f"g_sc{a}", align_bytes=64) for a in range(2)]
         g_words2 = keep.tile([P, S], U32, name="g_words2", align_bytes=64)
         g_parted = keep.tile([P, 2 * 2 * S], U8, name="g_parted", align_bytes=64)
-        g_sc2 = [keep.tile([P, S // 4], I32, name=f"g_sc2_{h}", align_bytes=64) for h in range(2)]
+        g_sc2 = keep.tile([P, S // 4], I32, name="g_sc2", align_bytes=64)
+        planes2 = [keep.tile([P, S // 4], I32, name=f"planes2_{h}", align_bytes=64) for h in range(2)]
 
-        nc.vector.memset(sc[0][:], 0)
-        nc.vector.memset(sc[1][:], 0)
+        nc.vector.memset(sc[:], 0)
         nc.gpsimd.memset(warm[:], 0.0)
-        nc.gpsimd.memset(sc2[:], 0)
-        nc.gpsimd.memset(g_sc2[1][:], 0)
         nc.gpsimd.memset(w4_sc[:], 0)
+        for h in range(2):
+            nc.gpsimd.memset(planes2[h][:], 0)
         nc.scalar.activation(out=warm[:], in_=warm[:], func=GELU)
 
-        def load_words(dst, row, eng):
-            eng.dma_start(out=dst[:], in_=row.rearrange("(p b) -> p b", b=4 * T).bitcast(I32))
+        def load_words(dst, row):
+            nc.sync.dma_start(out=dst[:], in_=row.rearrange("(p b) -> p b", b=4 * T).bitcast(I32))
 
-        def load_scales(dst, row, q, k0, row0, eng):
-            lo = WORD_BYTES + T * (row0 + 4 * q)
-            eng.dma_start(out=dst[32 * q + k0 : 32 * q + k0 + 4, :], in_=row[lo : lo + 4 * T].rearrange("(r b) -> r b", b=T).bitcast(I32))
-
+        nc.sync.dma_start(lst2[:], offs2)
+        end = WORD_BYTES + 32 * T
+        nc.sync.dma_start(out=sc2[:], in_=tab2[0, end - P * T : end].rearrange("(p t) -> p t", t=T).bitcast(I32))
         nc.sync.dma_start(lst[:], offs)
         for q in range(4):
-            load_scales(sc[0], tab[0], q, 0, 0, nc.sync)
+            lo = WORD_BYTES + 4 * q * T
+            nc.sync.dma_start(out=sc[32 * q : 32 * q + 4, :, :], in_=tab[:, lo : lo + 4 * T].rearrange("a (r t) -> r a t", t=T).bitcast(I32))
+        load_words(words2, tab2[0, 0:WORD_BYTES])
         nc.sync.dma_start(out=u_raw[:], in_=u.rearrange("(a p j) n -> p a j n", a=2, j=4))
-        load_words(words[0], tab[0, 0:WORD_BYTES], nc.sync)
+        load_words(words[0], tab[0, 0:WORD_BYTES])
+        load_words(words[1], tab[1, 0:WORD_BYTES])
+        nc.gpsimd.dma_start(out=w4[:], in_=w4_words.rearrange("a p c -> p a c").bitcast(I32))
         for q in range(4):
-            load_scales(sc[1], tab[1], q, 0, 0, nc.sync)
-        nc.sync.dma_start(lst2[:], offs2)
-        load_words(words2, tab2[0, 0:WORD_BYTES], nc.sync)
-        for h in range(2):
-            for q in range(4):
-                load_scales(sc2, tab2[0], q, 4 * h, 16 * h, nc.sync)
-        load_words(words[1], tab[1, 0:WORD_BYTES], nc.sync)
-        nc.scalar.dma_start(out=w4[:], in_=w4_words.rearrange("a p c -> p a c").bitcast(I32))
-        for q in range(4):
-            nc.scalar.dma_start(out=w4_sc[32 * q : 32 * q + 4, :, :], in_=w4_scales[:, 4 * q : 4 * q + 4, :].rearrange("a r n -> r a n").bitcast(I32))
-        nc.scalar.dma_start(out=bias[:], in_=b.rearrange("(p o) -> p o", o=1))
+            nc.gpsimd.dma_start(out=w4_sc[32 * q : 32 * q + 4, :, :], in_=w4_scales[:, 4 * q : 4 * q + 4, :].rearrange("a r n -> r a n").bitcast(I32))
+        nc.gpsimd.dma_start(out=bias[:], in_=b.rearrange("(p o) -> p o", o=1))
 
         for a in range(2):
             nc.scalar.copy(out=u_bf[:, a, :, :], in_=u_raw[:, a, :, :].rearrange("p j n -> p n j"))
@@ -85,18 +79,20 @@ def tile_list_tab48_gelu_kernel(tc, tab, w4_words, w4_scales, tab2, u, b, offs, 
         def gather(dst, window, offsets):
             nc.vector.tensor_copy(dst, window.indirect(offsets))
 
-        gather(g_sc[0][:], sc[0][:].bitcast(U8), lst[:])
-        gather(g_words[0][:], words[0][:].bitcast(U32), lst[:])
-        nc.vector.quantize_mx(out=u_codes[:].bitcast(FP8X4), scales=u_scales[:], in_=u_bf[:].rearrange("p a n j -> p (a n j)"))
+        gather(g_sc2[:].bitcast(U8), sc2[:].bitcast(U8), lst2[:])
+        for h in range(2):
+            for q in range(4):
+                r0 = 96 + 16 * h + 4 * q
+                nc.sync.dma_start(out=planes2[h][32 * q : 32 * q + 4, :], in_=g_sc2[r0 : r0 + 4, :])
+        for a in range(2):
+            gather(g_sc[a][:], sc[:, a, :].bitcast(U8), lst[:])
         gather(g_words2[:], words2[:].bitcast(U32), lst2[:])
-        gather(g_sc2[0][:].bitcast(U8), sc2[:].bitcast(U8), lst2[:])
-        for q in range(4):
-            nc.sync.dma_start(out=g_sc2[1][32 * q : 32 * q + 4, :], in_=g_sc2[0][32 * q + 4 : 32 * q + 8, :])
         nc.vector.tensor_copy(
             out=g_parted[:].bitcast(U16).rearrange("p (h n) -> p h n", h=2),
             in_=g_words2[:].bitcast(U16).rearrange("p (n h) -> p h n", h=2),
         )
-        gather(g_sc[1][:], sc[1][:].bitcast(U8), lst[:])
+        nc.vector.quantize_mx(out=u_codes[:].bitcast(FP8X4), scales=u_scales[:], in_=u_bf[:].rearrange("p a n j -> p (a n j)"))
+        gather(g_words[0][:], words[0][:].bitcast(U32), lst[:])
         pieces = ((0, 512), (512, 768), (768, 1024))
         for lo, hi in pieces:
             gather(g_words[1][:, lo:hi], words[1][:].bitcast(U32), lst[:, lo // 16 : hi // 16])
@@ -106,7 +102,7 @@ def tile_list_tab48_gelu_kernel(tc, tab, w4_words, w4_scales, tab2, u, b, offs, 
         w4_sc_u8 = w4_sc[:].rearrange("p a c -> p (a c)").bitcast(U8)
         acc = [psum.tile([M, hi - lo], F32, name=f"acc{lo}") for lo, hi in groups]
 
-        def mm_w4(i, a, start, stop):
+        def mm_w4(i, a):
             lo, hi = groups[i]
             nc.tensor.matmul_mx(
                 out=acc[i][:],
@@ -114,7 +110,7 @@ def tile_list_tab48_gelu_kernel(tc, tab, w4_words, w4_scales, tab2, u, b, offs, 
                 lhsT_scale=w4_sc_u8[:, M * a : M * a + M],
                 rhs=g_words[a][:, lo:hi].bitcast(FP8X4),
                 rhs_scale=g_sc[a][:, lo:hi],
-                start=start, stop=stop,
+                start=False, stop=(a == 1),
             )
 
         def mm_u(i, h):
@@ -124,19 +120,19 @@ def tile_list_tab48_gelu_kernel(tc, tab, w4_words, w4_scales, tab2, u, b, offs, 
                 lhsT=u_codes[:, M * h : M * h + M].bitcast(FP8X4),
                 lhsT_scale=u_scales[:, M * h : M * h + M],
                 rhs=g_parted[:, 2 * S * h + 2 * lo : 2 * S * h + 2 * hi].bitcast(FP4X4),
-                rhs_scale=g_sc2[h][:].bitcast(U8)[:, lo:hi],
-                start=False, stop=False,
+                rhs_scale=planes2[h][:].bitcast(U8)[:, lo:hi],
+                start=(h == 0), stop=False,
             )
 
-        for i in range(len(groups)):
-            mm_w4(i, 0, True, False)
         for h in range(2):
             for i in range(len(groups)):
                 mm_u(i, h)
+        for i in range(len(groups)):
+            mm_w4(i, 0)
         result = [keep.tile([M, hi - lo], F32, name=f"result{lo}") for lo, hi in pieces]
         for t, (p_lo, p_hi) in enumerate(pieces):
             for i, (lo, hi) in enumerate(groups):
                 if p_lo <= lo and hi <= p_hi:
-                    mm_w4(i, 1, False, True)
+                    mm_w4(i, 1)
                     nc.scalar.activation(out=result[t][:, lo - p_lo : hi - p_lo], in_=acc[i][:], func=GELU, bias=bias[:])
             nc.sync.dma_start(out=out[:, p_lo:p_hi], in_=result[t][:])

@@ -52,29 +52,29 @@ def tile_list_tab48_gelu_kernel(tc, tab, w4_words, w4_scales, tab2, u, b, offs, 
         nc.gpsimd.memset(w4_sc[:], 0)
         for h in range(2):
             nc.gpsimd.memset(planes2[h][:], 0)
-        nc.scalar.activation(out=warm[:], in_=warm[:], func=GELU)
 
         def load_words(dst, row):
             nc.sync.dma_start(out=dst[:], in_=row.rearrange("(p b) -> p b", b=4 * T).bitcast(I32))
 
         nc.sync.dma_start(lst2[:], offs2)
         end = WORD_BYTES + 32 * T
-        nc.sync.dma_start(out=sc2[:], in_=tab2[0, end - P * T : end].rearrange("(p t) -> p t", t=T).bitcast(I32))
+        nc.scalar.dma_start(out=sc2[:], in_=tab2[0, end - P * T : end].rearrange("(p t) -> p t", t=T).bitcast(I32))
+        nc.scalar.activation(out=warm[:], in_=warm[:], func=GELU)
+        load_words(words2, tab2[0, 0:WORD_BYTES])
         nc.sync.dma_start(lst[:], offs)
         for q in range(4):
             lo = WORD_BYTES + 4 * q * T
             nc.sync.dma_start(out=sc[32 * q : 32 * q + 4, :, :], in_=tab[:, lo : lo + 4 * T].rearrange("a (r t) -> r a t", t=T).bitcast(I32))
-        load_words(words2, tab2[0, 0:WORD_BYTES])
         nc.sync.dma_start(out=u_raw[:], in_=u.rearrange("(a p j) n -> p a j n", a=2, j=4))
         load_words(words[0], tab[0, 0:WORD_BYTES])
         load_words(words[1], tab[1, 0:WORD_BYTES])
-        nc.gpsimd.dma_start(out=w4[:], in_=w4_words.rearrange("a p c -> p a c").bitcast(I32))
-        for q in range(4):
-            nc.gpsimd.dma_start(out=w4_sc[32 * q : 32 * q + 4, :, :], in_=w4_scales[:, 4 * q : 4 * q + 4, :].rearrange("a r n -> r a n").bitcast(I32))
-        nc.gpsimd.dma_start(out=bias[:], in_=b.rearrange("(p o) -> p o", o=1))
-
         for a in range(2):
             nc.scalar.copy(out=u_bf[:, a, :, :], in_=u_raw[:, a, :, :].rearrange("p j n -> p n j"))
+
+        nc.scalar.dma_start(out=w4[:], in_=w4_words.rearrange("a p c -> p a c").bitcast(I32))
+        for q in range(4):
+            nc.scalar.dma_start(out=w4_sc[32 * q : 32 * q + 4, :, :], in_=w4_scales[:, 4 * q : 4 * q + 4, :].rearrange("a r n -> r a n").bitcast(I32))
+        nc.scalar.dma_start(out=bias[:], in_=b.rearrange("(p o) -> p o", o=1))
 
         def gather(dst, window, offsets):
             nc.vector.tensor_copy(dst, window.indirect(offsets))
@@ -84,13 +84,13 @@ def tile_list_tab48_gelu_kernel(tc, tab, w4_words, w4_scales, tab2, u, b, offs, 
             for q in range(4):
                 r0 = 96 + 16 * h + 4 * q
                 nc.sync.dma_start(out=planes2[h][32 * q : 32 * q + 4, :], in_=g_sc2[r0 : r0 + 4, :])
-        for a in range(2):
-            gather(g_sc[a][:], sc[:, a, :].bitcast(U8), lst[:])
         gather(g_words2[:], words2[:].bitcast(U32), lst2[:])
+        gather(g_sc[0][:], sc[:, 0, :].bitcast(U8), lst[:])
         nc.vector.tensor_copy(
             out=g_parted[:].bitcast(U16).rearrange("p (h n) -> p h n", h=2),
             in_=g_words2[:].bitcast(U16).rearrange("p (n h) -> p h n", h=2),
         )
+        gather(g_sc[1][:], sc[:, 1, :].bitcast(U8), lst[:])
         nc.vector.quantize_mx(out=u_codes[:].bitcast(FP8X4), scales=u_scales[:], in_=u_bf[:].rearrange("p a n j -> p (a n j)"))
         gather(g_words[0][:], words[0][:].bitcast(U32), lst[:])
         pieces = ((0, 512), (512, 768), (768, 1024))
@@ -135,4 +135,8 @@ def tile_list_tab48_gelu_kernel(tc, tab, w4_words, w4_scales, tab2, u, b, offs, 
                 if p_lo <= lo and hi <= p_hi:
                     mm_w4(i, 1)
                     nc.scalar.activation(out=result[t][:, lo - p_lo : hi - p_lo], in_=acc[i][:], func=GELU, bias=bias[:])
-            nc.sync.dma_start(out=out[:, p_lo:p_hi], in_=result[t][:])
+            if t < len(pieces) - 1:
+                nc.sync.dma_start(out=out[:, p_lo:p_hi], in_=result[t][:])
+            else:
+                for lo in (p_lo, p_lo + 128):
+                    nc.sync.dma_start(out=out[:, lo : lo + 128], in_=result[t][:, lo - p_lo : lo - p_lo + 128])

@@ -27,7 +27,7 @@ def tile_list_tab48_gelu_kernel(tc, tab, w4_words, w4_scales, tab2, u, b, offs, 
 
         lst = keep.tile([P, S // 16], U16, name="lst")
         lst2 = keep.tile([P, S // 16], U16, name="lst2")
-        sc = keep.tile([P, 2, T // 4], I32, name="sc", align_bytes=64)
+        sc = [keep.tile([P, T // 4], I32, name=f"sc{a}", align_bytes=64) for a in range(2)]
         words = [keep.tile([P, T], I32, name=f"words{a}", align_bytes=64) for a in range(2)]
         sc2 = keep.tile([P, T // 4], I32, name="sc2", align_bytes=64)
         words2 = keep.tile([P, T], I32, name="words2", align_bytes=64)
@@ -47,11 +47,11 @@ def tile_list_tab48_gelu_kernel(tc, tab, w4_words, w4_scales, tab2, u, b, offs, 
         g_sc2 = keep.tile([P, S // 4], I32, name="g_sc2", align_bytes=64)
         planes2 = [keep.tile([P, S // 4], I32, name=f"planes2_{h}", align_bytes=64) for h in range(2)]
 
-        nc.vector.memset(sc[:], 0)
-        nc.gpsimd.memset(warm[:], 0.0)
-        nc.gpsimd.memset(w4_sc[:], 0)
+        nc.vector.memset(warm[:], 0.0)
+        nc.vector.memset(sc[1][:], 0)
+        nc.vector.memset(w4_sc[:], 0)
         for h in range(2):
-            nc.gpsimd.memset(planes2[h][:], 0)
+            nc.vector.memset(planes2[h][:], 0)
 
         def load_words(dst, row):
             nc.sync.dma_start(out=dst[:], in_=row.rearrange("(p b) -> p b", b=4 * T).bitcast(I32))
@@ -60,11 +60,15 @@ def tile_list_tab48_gelu_kernel(tc, tab, w4_words, w4_scales, tab2, u, b, offs, 
         end = WORD_BYTES + 32 * T
         nc.scalar.dma_start(out=sc2[:], in_=tab2[0, end - P * T : end].rearrange("(p t) -> p t", t=T).bitcast(I32))
         nc.scalar.activation(out=warm[:], in_=warm[:], func=GELU)
-        load_words(words2, tab2[0, 0:WORD_BYTES])
         nc.sync.dma_start(lst[:], offs)
+        flat = tab.rearrange("a b -> (a b)")
         for q in range(4):
             lo = WORD_BYTES + 4 * q * T
-            nc.sync.dma_start(out=sc[32 * q : 32 * q + 4, :, :], in_=tab[:, lo : lo + 4 * T].rearrange("a (r t) -> r a t", t=T).bitcast(I32))
+            nc.sync.dma_start(out=sc[0][32 * q : 32 * q + 32, :], in_=flat[lo : lo + 32 * T].rearrange("(r t) -> r t", t=T).bitcast(I32))
+        load_words(words2, tab2[0, 0:WORD_BYTES])
+        for q in range(4):
+            lo = WORD_BYTES + 4 * q * T
+            nc.sync.dma_start(out=sc[1][32 * q : 32 * q + 4, :], in_=tab[1, lo : lo + 4 * T].rearrange("(r t) -> r t", t=T).bitcast(I32))
         nc.sync.dma_start(out=u_raw[:], in_=u.rearrange("(a p j) n -> p a j n", a=2, j=4))
         load_words(words[0], tab[0, 0:WORD_BYTES])
         load_words(words[1], tab[1, 0:WORD_BYTES])
@@ -84,18 +88,17 @@ def tile_list_tab48_gelu_kernel(tc, tab, w4_words, w4_scales, tab2, u, b, offs, 
             for q in range(4):
                 r0 = 96 + 16 * h + 4 * q
                 nc.sync.dma_start(out=planes2[h][32 * q : 32 * q + 4, :], in_=g_sc2[r0 : r0 + 4, :])
+        gather(g_sc[0][:], sc[0][:].bitcast(U8), lst[:])
         gather(g_words2[:], words2[:].bitcast(U32), lst2[:])
-        gather(g_sc[0][:], sc[:, 0, :].bitcast(U8), lst[:])
+        gather(g_sc[1][:], sc[1][:].bitcast(U8), lst[:])
         nc.vector.tensor_copy(
             out=g_parted[:].bitcast(U16).rearrange("p (h n) -> p h n", h=2),
             in_=g_words2[:].bitcast(U16).rearrange("p (n h) -> p h n", h=2),
         )
-        gather(g_sc[1][:], sc[:, 1, :].bitcast(U8), lst[:])
         nc.vector.quantize_mx(out=u_codes[:].bitcast(FP8X4), scales=u_scales[:], in_=u_bf[:].rearrange("p a n j -> p (a n j)"))
-        gather(g_words[0][:], words[0][:].bitcast(U32), lst[:])
         pieces = ((0, 512), (512, 768), (768, 1024))
-        for lo, hi in pieces:
-            gather(g_words[1][:, lo:hi], words[1][:].bitcast(U32), lst[:, lo // 16 : hi // 16])
+        for a, lo, hi in ((0, 0, 512), (1, 0, 512), (0, 512, 1024), (1, 512, 768), (1, 768, 1024)):
+            gather(g_words[a][:, lo:hi], words[a][:].bitcast(U32), lst[:, lo // 16 : hi // 16])
 
         groups = [(0, 512)] + [(lo, lo + 128) for lo in range(512, 1024, 128)]
         w4_u8 = w4[:].rearrange("p a c -> p (a c)").bitcast(U8)
@@ -127,10 +130,11 @@ def tile_list_tab48_gelu_kernel(tc, tab, w4_words, w4_scales, tab2, u, b, offs, 
         for h in range(2):
             for i in range(len(groups)):
                 mm_u(i, h)
-        for i in range(len(groups)):
-            mm_w4(i, 0)
         result = [keep.tile([M, hi - lo], F32, name=f"result{lo}") for lo, hi in pieces]
         for t, (p_lo, p_hi) in enumerate(pieces):
+            if t < 2:
+                for i in range(1) if t == 0 else range(1, len(groups)):
+                    mm_w4(i, 0)
             for i, (lo, hi) in enumerate(groups):
                 if p_lo <= lo and hi <= p_hi:
                     mm_w4(i, 1)

from contextlib import ExitStack

import concourse.mybir as mybir

K, L, M, T, S = 1024, 1024, 128, 2048, 1024
FLOPS = 2 * M * S * (K + L)

F32 = mybir.dt.float32
BF16 = mybir.dt.bfloat16
I32 = mybir.dt.int32
U32 = mybir.dt.uint32
U16 = mybir.dt.uint16
U8 = mybir.dt.uint8
FP8X4 = mybir.dt.float8_e4m3fn_x4
FP4X4 = mybir.dt.float4_e2m1fn_x4
GELU = mybir.ActivationFunctionType.Gelu_apprx_tanh

P = 128
WORD_BYTES = 512 * T


def tile_list_tab48_gelu_kernel(tc, tab, w4_words, w4_scales, tab2, u, b, offs, offs2, out):
    nc = tc.nc
    with ExitStack() as ctx:
        keep = ctx.enter_context(tc.tile_pool(name="keep", bufs=1))
        psum = ctx.enter_context(tc.psum_pool(name="psum", bufs=1))

        lst = keep.tile([P, S // 16], U16, name="lst")
        lst2 = keep.tile([P, S // 16], U16, name="lst2")
        sc = [keep.tile([P, T // 4], I32, name=f"sc{a}", align_bytes=64) for a in range(2)]
        words = [keep.tile([P, T], I32, name=f"words{a}", align_bytes=64) for a in range(2)]
        sc2 = keep.tile([P, T // 4], I32, name="sc2", align_bytes=64)
        words2 = keep.tile([P, T], I32, name="words2", align_bytes=64)
        u_raw = keep.tile([P, 2, 4, M], F32, name="u_raw", align_bytes=64)
        u_bf = keep.tile([P, 2, M, 4], BF16, name="u_bf", align_bytes=64)
        u_codes = keep.tile([P, 2 * M], U32, name="u_codes", align_bytes=64)
        u_scales = keep.tile([P, 2 * M], U8, name="u_scales", align_bytes=64)
        w4 = keep.tile([P, 2, M // 2], I32, name="w4", align_bytes=64)
        w4_sc = keep.tile([P, 2, M // 4], I32, name="w4_sc", align_bytes=64)
        bias = keep.tile([P, 1], F32, name="bias")
        warm = keep.tile([P, 1], F32, name="warm")

        g_words = [keep.tile([P, S], U32, name=f"g_words{a}", align_bytes=64) for a in range(2)]
        g_sc = [keep.tile([P, S], U8, name=f"g_sc{a}", align_bytes=64) for a in range(2)]
        g_words2 = keep.tile([P, S], U32, name="g_words2", align_bytes=64)
        g_parted = keep.tile([P, 2 * 2 * S], U8, name="g_parted", align_bytes=64)
        g_sc2 = keep.tile([P, S // 4], I32, name="g_sc2", align_bytes=64)
        planes2 = [keep.tile([P, S // 4], I32, name=f"planes2_{h}", align_bytes=64) for h in range(2)]

        nc.vector.memset(warm[:], 0.0)
        nc.vector.memset(sc[1][:], 0)
        nc.vector.memset(w4_sc[:], 0)
        for h in range(2):
            nc.vector.memset(planes2[h][:], 0)

        def load_words(dst, row):
            nc.sync.dma_start(out=dst[:], in_=row.rearrange("(p b) -> p b", b=4 * T).bitcast(I32))

        nc.sync.dma_start(lst2[:], offs2)
        end = WORD_BYTES + 32 * T
        nc.scalar.dma_start(out=sc2[:], in_=tab2[0, end - P * T : end].rearrange("(p t) -> p t", t=T).bitcast(I32))
        nc.scalar.activation(out=warm[:], in_=warm[:], func=GELU)
        nc.sync.dma_start(lst[:], offs)
        flat = tab.rearrange("a b -> (a b)")
        for q in range(4):
            lo = WORD_BYTES + 4 * q * T
            nc.sync.dma_start(out=sc[0][32 * q : 32 * q + 32, :], in_=flat[lo : lo + 32 * T].rearrange("(r t) -> r t", t=T).bitcast(I32))
        load_words(words2, tab2[0, 0:WORD_BYTES])
        for q in range(4):
            lo = WORD_BYTES + 4 * q * T
            nc.sync.dma_start(out=sc[1][32 * q : 32 * q + 4, :], in_=tab[1, lo : lo + 4 * T].rearrange("(r t) -> r t", t=T).bitcast(I32))
        nc.sync.dma_start(out=u_raw[:], in_=u.rearrange("(a p j) n -> p a j n", a=2, j=4))
        load_words(words[0], tab[0, 0:WORD_BYTES])
        load_words(words[1], tab[1, 0:WORD_BYTES])
        for a in range(2):
            nc.scalar.copy(out=u_bf[:, a, :, :], in_=u_raw[:, a, :, :].rearrange("p j n -> p n j"))

        nc.scalar.dma_start(out=w4[:], in_=w4_words.rearrange("a p c -> p a c").bitcast(I32))
        for q in range(4):
            nc.scalar.dma_start(out=w4_sc[32 * q : 32 * q + 4, :, :], in_=w4_scales[:, 4 * q : 4 * q + 4, :].rearrange("a r n -> r a n").bitcast(I32))
        nc.scalar.dma_start(out=bias[:], in_=b.rearrange("(p o) -> p o", o=1))

        def gather(dst, window, offsets):
            nc.vector.tensor_copy(dst, window.indirect(offsets))

        gather(g_sc2[:].bitcast(U8), sc2[:].bitcast(U8), lst2[:])
        for h in range(2):
            for q in range(4):
                r0 = 96 + 16 * h + 4 * q
                nc.sync.dma_start(out=planes2[h][32 * q : 32 * q + 4, :], in_=g_sc2[r0 : r0 + 4, :])
        gather(g_sc[0][:], sc[0][:].bitcast(U8), lst[:])
        gather(g_words2[:], words2[:].bitcast(U32), lst2[:])
        gather(g_sc[1][:], sc[1][:].bitcast(U8), lst[:])
        nc.vector.tensor_copy(
            out=g_parted[:].bitcast(U16).rearrange("p (h n) -> p h n", h=2),
            in_=g_words2[:].bitcast(U16).rearrange("p (n h) -> p h n", h=2),
        )
        nc.vector.quantize_mx(out=u_codes[:].bitcast(FP8X4), scales=u_scales[:], in_=u_bf[:].rearrange("p a n j -> p (a n j)"))
        pieces = ((0, 512), (512, 768), (768, 1024))
        for a, lo, hi in ((0, 0, 512), (1, 0, 512), (0, 512, 1024), (1, 512, 768), (1, 768, 1024)):
            gather(g_words[a][:, lo:hi], words[a][:].bitcast(U32), lst[:, lo // 16 : hi // 16])

        groups = [(0, 512)] + [(lo, lo + 128) for lo in range(512, 1024, 128)]
        w4_u8 = w4[:].rearrange("p a c -> p (a c)").bitcast(U8)
        w4_sc_u8 = w4_sc[:].rearrange("p a c -> p (a c)").bitcast(U8)
        acc = [psum.tile([M, hi - lo], F32, name=f"acc{lo}") for lo, hi in groups]

        def mm_w4(i, a):
            lo, hi = groups[i]
            nc.tensor.matmul_mx(
                out=acc[i][:],
                lhsT=w4_u8[:, 256 * a : 256 * a + 256].bitcast(FP4X4),
                lhsT_scale=w4_sc_u8[:, M * a : M * a + M],
                rhs=g_words[a][:, lo:hi].bitcast(FP8X4),
                rhs_scale=g_sc[a][:, lo:hi],
                start=False, stop=(a == 1),
            )

        def mm_u(i, h):
            lo, hi = groups[i]
            nc.tensor.matmul_mx(
                out=acc[i][:],
                lhsT=u_codes[:, M * h : M * h + M].bitcast(FP8X4),
                lhsT_scale=u_scales[:, M * h : M * h + M],
                rhs=g_parted[:, 2 * S * h + 2 * lo : 2 * S * h + 2 * hi].bitcast(FP4X4),
                rhs_scale=planes2[h][:].bitcast(U8)[:, lo:hi],
                start=(h == 0), stop=False,
            )

        for h in range(2):
            for i in range(len(groups)):
                mm_u(i, h)
        result = [keep.tile([M, hi - lo], F32, name=f"result{lo}") for lo, hi in pieces]
        for t, (p_lo, p_hi) in enumerate(pieces):
            if t < 2:
                for i in range(1) if t == 0 else range(1, len(groups)):
                    mm_w4(i, 0)
            for i, (lo, hi) in enumerate(groups):
                if p_lo <= lo and hi <= p_hi:
                    mm_w4(i, 1)
                    nc.scalar.activation(out=result[t][:, lo - p_lo : hi - p_lo], in_=acc[i][:], func=GELU, bias=bias[:])
            if t < len(pieces) - 1:
                nc.sync.dma_start(out=out[:, p_lo:p_hi], in_=result[t][:])
            else:
                for lo in (p_lo, p_lo + 128):
                    nc.sync.dma_start(out=out[:, lo : lo + 128], in_=result[t][:, lo - p_lo : lo - p_lo + 128])
